import numpy as np
import ml_dtypes

BF16 = ml_dtypes.bfloat16


def bf(x):
    return np.asarray(x, np.float32).astype(BF16)


def f32(x):
    return np.asarray(x, np.float32)


def f64(x):
    return np.asarray(x).astype(np.float64)


def striped(idx):
    return np.tile(idx.reshape(-1, 16).T, (8, 1))


def rows(idx, k):
    return np.tile(idx, (k, 1))


def look(tab, idx):
    return np.take_along_axis(f64(tab), rows(idx, len(tab)), axis=1)


K, S, D, V, N, M = 256, 2048, 2, 2048, 4096, 256


def setup_inputs():
    return {"tab": f32(0.7 * np.random.standard_normal((D, K, S))), "base": f32(np.random.standard_normal((K, V))), "w": bf(np.random.standard_normal((K, M)) / np.sqrt(K)), "offs": striped(np.random.randint(0, S, N))}


def reference(tab, base, w, offs):
    idx = offs[:16].T.reshape(-1)
    x = f64(base) + sum(look(tab[d], idx[d * V:(d + 1) * V]) for d in range(D))
    y = f64(w).T @ x
    return y

@@ -1,0 +1,75 @@
+import concourse.mybir as mybir
+
+P = 128
+LANES = 16
+PIECE = 512
+FLOPS = 2 * 256 * 256 * 2048
+
+F32, BF16, U16 = mybir.dt.float32, mybir.dt.bfloat16, mybir.dt.uint16
+ADD = mybir.AluOpType.add
+
+
+def tile_lookup_res_add_none_kernel(tc, tab, base, w, offs, out):
+    nc = tc.nc
+    stages, rows, codewords = tab.shape
+    columns = base.shape[1]
+    blocks = rows // P
+    halves = w.shape[1] // P
+    pieces = [slice(c, c + PIECE) for c in range(0, columns, PIECE)]
+    out_rows = out.rearrange("(h p) j -> p h j", p=P)
+
+    with (
+        tc.tile_pool(name="held", bufs=1) as held,
+        tc.psum_pool(name="psum", bufs=len(pieces)) as psum,
+    ):
+        offsets = held.tile(list(offs.shape), U16, name="offsets")
+        weights = held.tile([P, blocks, halves * P], BF16, name="weights")
+        window = [[held.tile([P, codewords], F32, name=f"window{d}{b}") for b in range(blocks)] for d in range(stages)]
+        start = [held.tile([P, columns], F32, name=f"start{b}") for b in range(blocks)]
+        partial = [held.tile([P, columns], F32, name=f"partial{b}") for b in range(blocks)]
+        x = [held.tile([P, columns], F32, name=f"x{b}") for b in range(blocks)]
+        rounded = [held.tile([P, columns], BF16, name=f"rounded{b}") for b in range(blocks)]
+        result = held.tile([P, halves, columns], F32, name="result")
+
+        def load_window(d, b):
+            nc.sync.dma_start(window[d][b][:], tab[d, b * P:(b + 1) * P, :])
+
+        def load_base(b, cols):
+            nc.sync.dma_start(start[b][:, cols], base[b * P:(b + 1) * P, cols])
+
+        def add_stage(d, b, cols):
+            first = d * columns // LANES
+            entries = offsets[:, first + cols.start // LANES:first + cols.stop // LANES]
+            before, after = ((start, partial), (partial, x))[d]
+            nc.vector.tensor_tensor(after[b][:, cols], window[d][b][:].indirect(entries), before[b][:, cols], ADD)
+
+        nc.sync.dma_start(offsets[:], offs)
+        load_window(0, 0)
+        for cols in pieces:
+            load_base(0, cols)
+        load_window(1, 0)
+        nc.sync.dma_start(weights[:], w.rearrange("(b p) m -> p b m", p=P))
+        load_window(0, 1)
+        load_base(1, pieces[0])
+        load_window(1, 1)
+        for cols in pieces[1:]:
+            load_base(1, cols)
+
+        for cols in pieces:
+            add_stage(0, 0, cols)
+        for cols in pieces:
+            add_stage(1, 0, cols)
+            nc.scalar.copy(rounded[0][:, cols], x[0][:, cols])
+
+        for cols in pieces:
+            add_stage(0, 1, cols)
+            add_stage(1, 1, cols)
+            nc.scalar.copy(rounded[1][:, cols], x[1][:, cols])
+            banks = [psum.tile([P, PIECE], F32, name=f"bank{h}") for h in range(halves)]
+            for b in range(blocks):
+                for h in range(halves):
+                    nc.tensor.matmul(banks[h][:], weights[:, b, h * P:(h + 1) * P], rounded[b][:, cols],
+                                     start=b == 0, stop=b == blocks - 1)
+            for h in range(halves):
+                nc.scalar.copy(result[:, h, cols], banks[h][:])
+            nc.sync.dma_start(out_rows[:, :, cols], result[:, :, cols])

@@ -2,11 +2,19 @@ import concourse.mybir as mybir
 
 P = 128
 LANES = 16
-PIECE = 512
+PIECE = 256
+BANKS = 8
 FLOPS = 2 * 256 * 256 * 2048
 
 F32, BF16, U16 = mybir.dt.float32, mybir.dt.bfloat16, mybir.dt.uint16
 ADD = mybir.AluOpType.add
+
+
+def doubling(first, total):
+    cuts = [slice(0, first)]
+    while cuts[-1].stop < total:
+        cuts.append(slice(cuts[-1].stop, 2 * cuts[-1].stop))
+    return cuts
 
 
 def tile_lookup_res_add_none_kernel(tc, tab, base, w, offs, out):
@@ -15,12 +23,14 @@ def tile_lookup_res_add_none_kernel(tc, tab, base, w, offs, out):
     columns = base.shape[1]
     blocks = rows // P
     halves = w.shape[1] // P
-    pieces = [slice(c, c + PIECE) for c in range(0, columns, PIECE)]
+    fine = columns - 2 * PIECE
+    edges = [*range(0, fine, PIECE), *range(fine, columns + 1, PIECE // 2)]
+    pieces = [slice(a, z) for a, z in zip(edges, edges[1:])]
     out_rows = out.rearrange("(h p) j -> p h j", p=P)
 
     with (
         tc.tile_pool(name="held", bufs=1) as held,
-        tc.psum_pool(name="psum", bufs=len(pieces)) as psum,
+        tc.psum_pool(name="psum", bufs=BANKS // halves) as psum,
     ):
         offsets = held.tile(list(offs.shape), U16, name="offsets")
         weights = held.tile([P, blocks, halves * P], BF16, name="weights")
@@ -43,33 +53,48 @@ def tile_lookup_res_add_none_kernel(tc, tab, base, w, offs, out):
             before, after = ((start, partial), (partial, x))[d]
             nc.vector.tensor_tensor(after[b][:, cols], window[d][b][:].indirect(entries), before[b][:, cols], ADD)
 
-        nc.sync.dma_start(offsets[:], offs)
-        load_window(0, 0)
-        for cols in pieces:
-            load_base(0, cols)
-        load_window(1, 0)
-        nc.sync.dma_start(weights[:], w.rearrange("(b p) m -> p b m", p=P))
-        load_window(0, 1)
-        load_base(1, pieces[0])
-        load_window(1, 1)
-        for cols in pieces[1:]:
-            load_base(1, cols)
-
-        for cols in pieces:
-            add_stage(0, 0, cols)
-        for cols in pieces:
-            add_stage(1, 0, cols)
-            nc.scalar.copy(rounded[0][:, cols], x[0][:, cols])
-
-        for cols in pieces:
-            add_stage(0, 1, cols)
-            add_stage(1, 1, cols)
-            nc.scalar.copy(rounded[1][:, cols], x[1][:, cols])
-            banks = [psum.tile([P, PIECE], F32, name=f"bank{h}") for h in range(halves)]
+        def multiply(cols):
+            cast = nc.vector.tensor_copy if cols.stop == columns else nc.scalar.copy
+            cast(rounded[1][:, cols], x[1][:, cols])
+            banks = [psum.tile([P, cols.stop - cols.start], F32, name=f"bank{h}") for h in range(halves)]
             for b in range(blocks):
                 for h in range(halves):
                     nc.tensor.matmul(banks[h][:], weights[:, b, h * P:(h + 1) * P], rounded[b][:, cols],
                                      start=b == 0, stop=b == blocks - 1)
-            for h in range(halves):
-                nc.scalar.copy(result[:, h, cols], banks[h][:])
+            return banks
+
+        def store(cols, banks):
+            second = nc.vector.tensor_copy if cols in pieces[-2:] else nc.scalar.copy
+            nc.scalar.copy(result[:, 0, cols], banks[0][:])
+            second(result[:, 1, cols], banks[1][:])
             nc.sync.dma_start(out_rows[:, :, cols], result[:, :, cols])
+
+        load_window(0, 0)
+        nc.sync.dma_start(offsets[:], offs)
+        for cols in doubling(PIECE, columns):
+            load_base(0, cols)
+        load_window(1, 0)
+        load_window(0, 1)
+        first_base, *later_base = doubling(2 * PIECE, columns)
+        load_base(1, first_base)
+        load_window(1, 1)
+        nc.sync.dma_start(weights[:], w.rearrange("(b p) m -> p b m", p=P))
+        for cols in later_base:
+            load_base(1, cols)
+
+        for cols in doubling(PIECE, columns):
+            add_stage(0, 0, cols)
+        for cols in doubling(columns // 2, columns):
+            add_stage(1, 0, cols)
+            nc.scalar.copy(rounded[0][:, cols], x[0][:, cols])
+
+        add_stage(0, 1, pieces[0])
+        products = []
+        for k, cols in enumerate(pieces):
+            if k + 1 < len(pieces):
+                add_stage(0, 1, pieces[k + 1])
+            add_stage(1, 1, cols)
+            products.append(multiply(cols))
+            if k > 0:
+                store(pieces[k - 1], products[k - 1])
+        store(pieces[-1], products[-1])

@@ -54,8 +54,7 @@ def tile_lookup_res_add_none_kernel(tc, tab, base, w, offs, out):
             nc.vector.tensor_tensor(after[b][:, cols], window[d][b][:].indirect(entries), before[b][:, cols], ADD)
 
         def multiply(cols):
-            cast = nc.vector.tensor_copy if cols.stop == columns else nc.scalar.copy
-            cast(rounded[1][:, cols], x[1][:, cols])
+            nc.scalar.copy(rounded[1][:, cols], x[1][:, cols])
             banks = [psum.tile([P, cols.stop - cols.start], F32, name=f"bank{h}") for h in range(halves)]
             for b in range(blocks):
                 for h in range(halves):
@@ -64,7 +63,7 @@ def tile_lookup_res_add_none_kernel(tc, tab, base, w, offs, out):
             return banks
 
         def store(cols, banks):
-            second = nc.vector.tensor_copy if cols in pieces[-2:] else nc.scalar.copy
+            second = nc.vector.tensor_copy if cols in pieces[-3:] else nc.scalar.copy
             nc.scalar.copy(result[:, 0, cols], banks[0][:])
             second(result[:, 1, cols], banks[1][:])
             nc.sync.dma_start(out_rows[:, :, cols], result[:, :, cols])

import concourse.mybir as mybir

P = 128
LANES = 16
PIECE = 256
BANKS = 8
FLOPS = 2 * 256 * 256 * 2048

F32, BF16, U16 = mybir.dt.float32, mybir.dt.bfloat16, mybir.dt.uint16
ADD = mybir.AluOpType.add


def doubling(first, total):
    cuts = [slice(0, first)]
    while cuts[-1].stop < total:
        cuts.append(slice(cuts[-1].stop, 2 * cuts[-1].stop))
    return cuts


def tile_lookup_res_add_none_kernel(tc, tab, base, w, offs, out):
    nc = tc.nc
    stages, rows, codewords = tab.shape
    columns = base.shape[1]
    blocks = rows // P
    halves = w.shape[1] // P
    fine = columns - 2 * PIECE
    edges = [*range(0, fine, PIECE), *range(fine, columns + 1, PIECE // 2)]
    pieces = [slice(a, z) for a, z in zip(edges, edges[1:])]
    out_rows = out.rearrange("(h p) j -> p h j", p=P)

    with (
        tc.tile_pool(name="held", bufs=1) as held,
        tc.psum_pool(name="psum", bufs=BANKS // halves) as psum,
    ):
        offsets = held.tile(list(offs.shape), U16, name="offsets")
        weights = held.tile([P, blocks, halves * P], BF16, name="weights")
        window = [[held.tile([P, codewords], F32, name=f"window{d}{b}") for b in range(blocks)] for d in range(stages)]
        start = [held.tile([P, columns], F32, name=f"start{b}") for b in range(blocks)]
        partial = [held.tile([P, columns], F32, name=f"partial{b}") for b in range(blocks)]
        x = [held.tile([P, columns], F32, name=f"x{b}") for b in range(blocks)]
        rounded = [held.tile([P, columns], BF16, name=f"rounded{b}") for b in range(blocks)]
        result = held.tile([P, halves, columns], F32, name="result")

        def load_window(d, b):
            nc.sync.dma_start(window[d][b][:], tab[d, b * P:(b + 1) * P, :])

        def load_base(b, cols):
            nc.sync.dma_start(start[b][:, cols], base[b * P:(b + 1) * P, cols])

        def add_stage(d, b, cols):
            first = d * columns // LANES
            entries = offsets[:, first + cols.start // LANES:first + cols.stop // LANES]
            before, after = ((start, partial), (partial, x))[d]
            nc.vector.tensor_tensor(after[b][:, cols], window[d][b][:].indirect(entries), before[b][:, cols], ADD)

        def multiply(cols):
            nc.scalar.copy(rounded[1][:, cols], x[1][:, cols])
            banks = [psum.tile([P, cols.stop - cols.start], F32, name=f"bank{h}") for h in range(halves)]
            for b in range(blocks):
                for h in range(halves):
                    nc.tensor.matmul(banks[h][:], weights[:, b, h * P:(h + 1) * P], rounded[b][:, cols],
                                     start=b == 0, stop=b == blocks - 1)
            return banks

        def store(cols, banks):
            second = nc.vector.tensor_copy if cols in pieces[-3:] else nc.scalar.copy
            nc.scalar.copy(result[:, 0, cols], banks[0][:])
            second(result[:, 1, cols], banks[1][:])
            nc.sync.dma_start(out_rows[:, :, cols], result[:, :, cols])

        load_window(0, 0)
        nc.sync.dma_start(offsets[:], offs)
        for cols in doubling(PIECE, columns):
            load_base(0, cols)
        load_window(1, 0)
        load_window(0, 1)
        first_base, *later_base = doubling(2 * PIECE, columns)
        load_base(1, first_base)
        load_window(1, 1)
        nc.sync.dma_start(weights[:], w.rearrange("(b p) m -> p b m", p=P))
        for cols in later_base:
            load_base(1, cols)

        for cols in doubling(PIECE, columns):
            add_stage(0, 0, cols)
        for cols in doubling(columns // 2, columns):
            add_stage(1, 0, cols)
            nc.scalar.copy(rounded[0][:, cols], x[0][:, cols])

        add_stage(0, 1, pieces[0])
        products = []
        for k, cols in enumerate(pieces):
            if k + 1 < len(pieces):
                add_stage(0, 1, pieces[k + 1])
            add_stage(1, 1, cols)
            products.append(multiply(cols))
            if k > 0:
                store(pieces[k - 1], products[k - 1])
        store(pieces[-1], products[-1])
